import numpy as np, ml_dtypes
CORES = [16,32,48,64,80]
N = 5
import mx_ref
NC, ROOT = 512, 1
C = np.float32(0.037)
BF = ml_dtypes.bfloat16
def cut(t, i, w=512):
    return t[:, w * i:w * i + w]
def tile(rs):
    return np.stack(rs, axis=2).reshape(128, -1).astype(BF)
def pick(b):
    s = np.zeros((128, 128, 4), np.float32)
    s[np.arange(128), np.arange(128), b] = 1.0
    return mx_ref.quantize(s.reshape(128, 512).astype(BF))
def pk(c, s, i=0):
    return (np.ascontiguousarray(c[:, 512 * i:512 * i + 512]), mx_ref.live(s[:, 128 * i:128 * i + 128]))
def inputs(rng, e, E):
    def f(*shape):
        v = (rng.standard_normal(shape, dtype=np.float32) * np.exp2(rng.integers(-2, 3, shape[:-1] + (1,)))).astype(BF)
        return mx_ref.spread((v.astype(np.float32) * np.exp2(rng.integers(-E, E + 1, shape[:-2] + (1, 1))).astype(np.float32)).astype(BF), rng, e)
    def packed(k):
        c = np.zeros((N, 128, k * 512), np.uint8); s = np.zeros((N, 128, k * 128), np.uint8)
        for r in range(N):
            for i in range(k):
                a, b = mx_ref.quantize(f(128, 512)); c[r][:, 512 * i:512 * i + 512] = a; s[r][:, 128 * i:128 * i + 128] = mx_ref.plane(b, rng)
        return c, s
    d = {}
    d["wc"], d["ws"] = packed(1)
    d["a"] = f(N, 128, 512)
    d["bb"] = f(N, 128, 4 * 512)
    d["x"] = f(N, 128, 4 * NC)
    return d
def setup_inputs(rng):
    return inputs(rng, 0, 0)
def setup_inputs_blocks(rng):
    return inputs(rng, 2, 0)
def setup_inputs_wide(rng):
    return inputs(rng, 0, 3)
def reference(wc, ws, a, bb, x):
    S = [pick(t) for t in range(4)]; A = mx_ref.quantize(a[ROOT])
    V = [mx_ref.quantize(tile([mx_ref.matmul(S[t], pk(wc[j], ws[j])) + mx_ref.matmul(mx_ref.quantize(cut(bb[j], t)), A) * C for t in range(4)])) for j in range(N)]
    y = np.zeros((N, 128, N * NC), np.float32)
    for r in range(N):
        X = mx_ref.quantize(x[r])
        for j in range(N):
            y[r][:, NC * j:NC * j + NC] = mx_ref.matmul(V[j], X)
    return {"y": y}

import numpy as np
from concourse.bass import DstId, RemoteDMATransfer
from concourse.mybir import dt, AluOpType, ActivationFunctionType

N = 5
NC = 512
M = 128
HALF = NC // 2
BANK = 512
BANKS = 8
C = float(np.float32(0.037))
ZW = 520

CODE, PLANE = "float8_e4m3fn_x4", "uint8"
SCRATCH = {
    "z": ("sbuf", [128, ZW], "bfloat16"),
    "ta": ("sbuf", [128, 4 * M], "bfloat16"),
    "tb": ("sbuf", [128, 16 * M], "bfloat16"),
    "tx": ("sbuf", [128, 4 * NC], "bfloat16"),
    "qs": ("sbuf", [128, 4 * M], CODE), "ss": ("sbuf", [128, 4 * M], PLANE),
    "qa": ("sbuf", [128, M], CODE), "sa": ("sbuf", [128, M], PLANE),
    "qb": ("sbuf", [128, 4 * M], CODE), "sb": ("sbuf", [128, 4 * M], PLANE),
    "qx": ("sbuf", [128, NC], CODE), "sx": ("sbuf", [128, NC], PLANE),
    "qw": ("sbuf", [128, M], CODE), "sw": ("sbuf", [128, M], PLANE),
    "qv": ("sbuf", [128, N * M], CODE), "sv": ("sbuf", [128, N * M], PLANE),
    "sc": ("sbuf", [128, 4 * M], "float32"),
    "tv": ("sbuf", [128, 4 * M], "bfloat16"),
    "yo": ("sbuf", [128, N * NC], "float32"),
    "ps": ("psum", [128, BANKS * BANK], "float32"),
}
SEMAPHORES = (["ld_a", "ld_b", "ld_x", "ld_w", "z0", "z1", "q_s", "q_a", "q_b", "q_x", "q_v", "d", "v", "arr_a", "loc", "st", "st2"]
              + ["m%d" % b for b in range(4)] + ["s%d" % b for b in range(4)]
              + ["arr%d" % j for j in range(N)]
              + ["h%d" % h for h in range(2 * N)] + ["c%d" % h for h in range(2 * N)])


def rank_program(g, core, T, topo):
    rank = T.rank_of(core)
    if rank is None:
        return
    root = T.root
    is_root = rank == root
    sem = T.sem

    line = [(root + 1 + k) % N for k in range(N - 1)]
    if is_root:
        dests = line
    else:
        k = line.index(rank)
        dests = [line[(k - 1 - m) % (N - 1)] for m in range(N - 2)] + [root]
    if is_root:
        order = [root] + line
    else:
        def when(j):
            kj = line.index(j)
            return kj + (kj - 1 - line.index(rank)) % (N - 1), kj
        order = [rank, root] + sorted([j for j in line if j != rank], key=when)

    def bank(i, n):
        return T.ps[:, BANK * i:BANK * i + n]

    def cols(t, i, w=M):
        return t[:, w * i:w * i + w]

    def send(code, plane, ranks, arrived):
        cores = [T.cores[r] for r in ranks]
        mask = topo.mask(core, cores[0])
        for c in cores[1:]:
            mask &= topo.mask(core, c)
        ids = []
        for c in cores:
            rid, pid, _ = topo.addr(c)
            ids.append(DstId(rid=rid, pnc=pid))
        for ap in (plane, code.bitcast(dt.uint8)):
            g.remote_dma_fused([RemoteDMATransfer(dst_ids=ids, dma_engine_mask=mask, remote_sem=arrived,
                                                  srcs=[ap], dsts=[ap] * len(ids))], local_sem=sem.loc)
        return 2 * bin(mask).count("1")

    per_send = 2 * bin(topo.mask(core, T.cores[(rank + 1) % N])).count("1")

    if is_root:
        g.sync.dma_start(T.ta[:], T.a[:]).then_inc(sem.ld_a, 16)
        q2 = g.sync
    else:
        q2 = g.scalar
    q2.dma_start(T.qw[:].bitcast(dt.uint8), T.wc[:]).then_inc(sem.ld_w, 16)
    q2.dma_start(T.sw[:], T.ws[:]).then_inc(sem.ld_w, 16)
    g.sync.dma_start(T.tb[:], T.bb[:]).then_inc(sem.ld_b, 16)
    q2.dma_start(T.tx[:], T.x[:]).then_inc(sem.ld_x, 16)

    def quant_s():
        g.vector.wait_ge(sem.z1, 1)
        for b in range(4):
            g.vector.quantize_mx(cols(T.qs, b), cols(T.ss, b), T.z[:, 3 - b:3 - b + 4 * M]).then_inc(sem.q_s, 1)

    g.vector.memset(T.z[:], 0.0).then_inc(sem.z0, 1)
    if is_root:
        g.vector.wait_ge(sem.ld_a, 16)
        g.vector.quantize_mx(T.qa[:], T.sa[:], T.ta[:]).then_inc(sem.q_a, 1)
    quant_s()
    g.vector.wait_ge(sem.ld_b, 16)
    g.vector.quantize_mx(T.qb[:], T.sb[:], T.tb[:]).then_inc(sem.q_b, 1)
    if not is_root:
        g.vector.wait_ge(sem.ld_x, 16)
        g.vector.quantize_mx(T.qx[:], T.sx[:], T.tx[:]).then_inc(sem.q_x, 1)

    g.wait_ge(sem.z0, 1)
    g.affine_select(T.z[:], T.z[:], [[1, ZW]], AluOpType.not_equal, 1.0, -3, -4).then_inc(sem.z1, 1)
    left = 0
    if is_root:
        g.wait_ge(sem.q_a, 1)
        left += send(T.qa[:], T.sa[:], line, sem.arr_a)
    g.wait_ge(sem.q_v, 1)
    left += send(cols(T.qv, rank), cols(T.sv, rank), dests, sem["arr%d" % rank])
    g.wait_ge(sem.loc, left)

    g.tensor.wait_ge(sem.q_s, 4)
    g.tensor.wait_ge(sem.ld_w, 32)
    for b in range(4):
        g.tensor.matmul_mx(bank(b, M), cols(T.qs, b), cols(T.ss, b), T.qw[:], T.sw[:], True, True).then_inc(sem.d, 1)
    g.tensor.wait_ge(sem.q_b, 1)
    if is_root:
        g.tensor.wait_ge(sem.q_a, 1)
    else:
        g.tensor.wait_ge(sem.arr_a, per_send)
    for b in range(4):
        g.tensor.matmul_mx(bank(4 + b, M), cols(T.qb, b), cols(T.sb, b), T.qa[:], T.sa[:], True, True).then_inc(sem["m%d" % b], 1)

    for b in range(4):
        g.scalar.wait_ge(sem["m%d" % b], 1)
        g.scalar.activation(cols(T.sc, b), bank(4 + b, M), ActivationFunctionType.Copy, scale=C).then_inc(sem["s%d" % b], 1)
    g.vector.wait_ge(sem.d, 4)
    for b in range(4):
        g.vector.wait_ge(sem["s%d" % b], 1)
        g.vector.tensor_tensor(T.tv[:, b:4 * M:4], bank(b, M), cols(T.sc, b), AluOpType.add).then_inc(sem.v, 1)
    g.vector.wait_ge(sem.v, 4)
    g.vector.quantize_mx(cols(T.qv, rank), cols(T.sv, rank), T.tv[:]).then_inc(sem.q_v, 1)
    if is_root:
        g.vector.wait_ge(sem.ld_x, 16)
        g.vector.quantize_mx(T.qx[:], T.sx[:], T.tx[:]).then_inc(sem.q_x, 1)

    g.tensor.wait_ge(sem.q_x, 1)
    for i, j in enumerate(order):
        if i == 0:
            g.tensor.wait_ge(sem.q_v, 1)
        else:
            g.tensor.wait_ge(sem["arr%d" % j], per_send)
        for e in range(2):
            h = 2 * i + e
            if h >= BANKS:
                g.tensor.wait_ge(sem["c%d" % (h - BANKS)], 1)
            g.tensor.matmul_mx(bank(h % BANKS, HALF), cols(T.qv, j), cols(T.sv, j),
                               cols(T.qx, e, HALF), cols(T.sx, e, HALF), True, True).then_inc(sem["h%d" % h], 1)
        last = i == N - 1
        lo, mid, hi = NC * j, NC * j + HALF, NC * j + NC
        h = 2 * i
        g.vector.wait_ge(sem["h%d" % h], 1)
        g.vector.tensor_copy(T.yo[:, lo:mid], bank(h % BANKS, HALF)).then_inc(sem["c%d" % h], 1)
        g.scalar.wait_ge(sem["h%d" % (h + 1)], 1)
        g.scalar.activation(T.yo[:, mid:hi], bank((h + 1) % BANKS, HALF), ActivationFunctionType.Copy).then_inc(sem["c%d" % (h + 1)], 1)
        g.sync.wait_ge(sem["c%d" % h], 1)
        if last:
            g.scalar.wait_ge(sem["c%d" % (h + 1)], 1)
            g.sync.dma_start(T.y[:, lo:mid], T.yo[:, lo:mid]).then_inc(sem.st, 16)
            g.scalar.dma_start(T.y[:, mid:hi], T.yo[:, mid:hi]).then_inc(sem.st2, 16)
        else:
            g.sync.wait_ge(sem["c%d" % (h + 1)], 1)
            g.sync.dma_start(T.y[:, lo:hi], T.yo[:, lo:hi]).then_inc(sem.st, 16)
    g.sync.wait_ge(sem.st, 16 * N)
    g.scalar.wait_ge(sem.st2, 16)
